import numpy as np
import ml_dtypes


def mxq(x, axis, fmt="e4m3"):
    dtype, down = {"e4m3": (ml_dtypes.float8_e4m3fn, 7), "e5m2": (ml_dtypes.float8_e5m2, 14)}[fmt]
    v = np.moveaxis(np.asarray(x, np.float32).astype(ml_dtypes.bfloat16).astype(np.float64), axis, -1)
    blocks = v.reshape(v.shape[:-1] + (-1, 32))
    amax = np.abs(blocks).max(-1, keepdims=True)
    byte = np.maximum(np.where(amax > 0, np.frexp(amax)[1] - 1 + 127, 0) - down, 1)
    scale = np.exp2(byte - 127.0)
    codes = (blocks / scale).astype(np.float32).astype(dtype).astype(np.float64)
    return np.moveaxis((codes * scale).reshape(v.shape), -1, axis)


WIDE = False


def mx_kscale(k):
    if not WIDE:
        return np.ones(k)
    levels = np.array([10, -10, 5, -5, 0])
    if k % 512:
        return np.exp2(np.random.permutation(np.resize(levels, k // 32))).repeat(32)
    a = np.empty((k // 512, 16))
    for p in range(k // 512):
        a[p, :8] = np.random.permutation(np.resize(levels, 8))
        for g in range(8):
            far = levels[np.abs(levels - a[p, g]) >= 10]
            a[p, g + 8] = far[np.random.randint(len(far))]
    return np.exp2(a.ravel()).repeat(32)


BF16 = ml_dtypes.bfloat16


def bf(x):
    return np.asarray(x, np.float32).astype(BF16)


def f64(x):
    return np.asarray(x).astype(np.float64)


N, D, C, F = 4096, 512, 512, 512


def clip_to_radius(delta, radius):
    nrm = np.sqrt(np.sum(delta * delta, axis=-1))
    scale = np.minimum(1.0, radius / nrm)
    return delta * scale[:, None]


def drop_parallel(e, direction):
    coef = np.sum(e * direction, axis=-1) / np.sum(direction * direction, axis=-1)
    return e - coef[:, None] * direction


def draw0():
    s, r, t = mx_kscale(D), mx_kscale(C), mx_kscale(F)
    return {
        "x": bf(np.random.standard_normal((N, D)) * s),
        "cond": bf(np.random.standard_normal((N, C)) * r),
        "w1": bf(np.random.standard_normal((D, F)) / np.sqrt(D) / s[:, None] * t),
        "wc": bf(np.random.standard_normal((C, F)) / np.sqrt(C) / r[:, None]),
        "w2": bf(np.random.standard_normal((F, D)) / np.sqrt(F) / t[:, None]),
        "delta_prev": bf(0.7 * np.random.standard_normal((N, D))),
        "radius": bf(np.random.uniform(0.35, 1.06, N) * np.sqrt(D)),
    }


def core(x, cond, w1, wc, w2, delta_prev, radius):
    u = mxq(f64(x), 1, "e4m3") @ mxq(f64(w1), 0, "e4m3")
    a = mxq(f64(cond), 1, "e4m3") @ mxq(f64(wc), 0, "e4m3")
    hc = u * (1.0 + np.tanh(a))
    hu = u
    w2q = mxq(f64(w2), 0, "e4m3")
    dc = mxq(hc, 1, "e4m3") @ w2q
    du = mxq(hu, 1, "e4m3") @ w2q
    delta = (dc - du) - 0.5 * f64(delta_prev)
    e = clip_to_radius(delta, f64(radius))
    orth = drop_parallel(e, dc)
    return dc + 3.0 * orth


def e4m3fn_bytes(y):
    return np.clip(np.asarray(y, np.float64), -448.0, 448.0).astype(np.float32).astype(ml_dtypes.float8_e4m3fn).view(np.uint8)


def e4m3fn_values(b):
    return np.asarray(b, np.uint8).view(ml_dtypes.float8_e4m3fn).astype(np.float64)


def setup_inputs():
    d = draw0()
    x0 = np.asarray(d['x']).astype(np.float64)
    s = (np.max(np.abs(x0), axis=(0,), keepdims=True) / 448.0).astype(np.float32)
    out = {}
    for k, v in d.items():
        if k == 'x':
            out['x_bytes'] = e4m3fn_bytes(x0 / s.astype(np.float64))
            out['x_scale'] = s
        else:
            out[k] = v
    return out


def reference(x_bytes, x_scale, cond, w1, wc, w2, delta_prev, radius):
    return core(e4m3fn_values(x_bytes) * x_scale.astype(np.float64), cond, w1, wc, w2, delta_prev, radius)

@@ -1,0 +1,358 @@
+from contextlib import ExitStack
+
+import concourse.mybir as mybir
+from concourse.masks import make_identity
+
+N, D, C, F = 4096, 512, 512, 512
+FLOPS = 4 * 2 * N * D * F
+
+F32 = mybir.dt.float32
+BF16 = mybir.dt.bfloat16
+U32 = mybir.dt.uint32
+U8 = mybir.dt.uint8
+FP8 = mybir.dt.float8_e4m3fn
+FP8X4 = mybir.dt.float8_e4m3fn_x4
+ALU = mybir.AluOpType
+ACT = mybir.ActivationFunctionType
+
+P = 128
+T = 4
+TILES = N // P
+
+X_CHUNKS = (1, 1, 2, 4, 8, 8, 8)
+C_CHUNKS = (1, 1, 2, 4, 8, 8, 8)
+DP_CHUNKS = (2, 2, 4, 8, 8, 8)
+
+
+def tile_adaptiveprojectedguidancehead_t_kernel(
+    tc, x_bytes, x_scale, cond, w1, wc, w2, delta_prev, radius, out
+):
+    nc = tc.nc
+    with ExitStack() as ctx:
+        keep = ctx.enter_context(tc.tile_pool(name="keep", bufs=1))
+        work = ctx.enter_context(tc.tile_pool(name="work", bufs=3))
+        ps_xt = ctx.enter_context(tc.psum_pool(name="ps_xt", bufs=1))
+        ps_u = ctx.enter_context(tc.psum_pool(name="ps_u", bufs=2))
+        ps_a = ctx.enter_context(tc.psum_pool(name="ps_a", bufs=1))
+        ps_dc = ctx.enter_context(tc.psum_pool(name="ps_dc", bufs=3))
+        ps_q = ctx.enter_context(tc.psum_pool(name="ps_q", bufs=1))
+
+        xv = x_bytes.rearrange("(p i) k -> p i k", i=TILES)
+        cv = cond.rearrange("(p i) k -> p i k", i=TILES)
+        dv = delta_prev.rearrange("(p i) k -> p i k", i=TILES)
+        ov = out.rearrange("(p i) k -> p i k", i=TILES)
+
+        ctx.enter_context(tc.manual_schedule())
+
+        def chunk_tiles(sizes, dtype, tag):
+            where = []
+            chunks = []
+            first = 0
+            for n, size in enumerate(sizes):
+                chunk = keep.tile([P, size, D], dtype, name=tag + str(n))
+                chunks.append((chunk, first, size))
+                for j in range(size):
+                    where.append((chunk, j))
+                first += size
+            return chunks, where
+
+        x_chunks, x_at = chunk_tiles(X_CHUNKS, U8, "xb")
+        c_chunks, c_at = chunk_tiles(C_CHUNKS, BF16, "cd")
+        d_chunks, d_at = chunk_tiles(DP_CHUNKS, BF16, "dp")
+
+        def load(chunks, view, n):
+            chunk, first, size = chunks[n]
+            nc.sync.dma_start(out=chunk[:], in_=view[:, first : first + size, :])
+
+        def load_weight(w, tag):
+            raw = keep.tile([P, T, F], BF16, name=tag + "_raw")
+            nc.sync.dma_start(out=raw[:], in_=w.rearrange("(p j) n -> p j n", j=T))
+            return raw
+
+        scale = keep.tile([P, D], F32, name="scale")
+        rad = keep.tile([P, TILES], BF16, name="rad")
+
+        load(c_chunks, cv, 0)
+        load(x_chunks, xv, 0)
+        wc_raw = load_weight(wc, "wc")
+        nc.sync.dma_start(
+            out=scale[:], in_=x_scale.rearrange("o k -> (o k)").partition_broadcast(P)
+        )
+        w1_raw = load_weight(w1, "w1")
+        load(c_chunks, cv, 1)
+        load(x_chunks, xv, 1)
+        w2_raw = load_weight(w2, "w2")
+        load(c_chunks, cv, 2)
+        load(x_chunks, xv, 2)
+        load(d_chunks, dv, 0)
+        nc.sync.dma_start(out=rad[:], in_=radius.rearrange("(p i) -> p i", i=TILES))
+        load(c_chunks, cv, 3)
+        load(x_chunks, xv, 3)
+        load(d_chunks, dv, 1)
+        load(d_chunks, dv, 2)
+        for n in range(4, 7):
+            load(c_chunks, cv, n)
+            load(x_chunks, xv, n)
+            load(d_chunks, dv, n - 1)
+
+        ident = keep.tile([P, P], F32, name="ident")
+        make_identity(nc, ident[:])
+        expo = keep.tile([P, 2], F32, name="expo")
+        nc.gpsimd.memset(expo[:, 0:1], -0.5)
+        nc.gpsimd.memset(expo[:, 1:2], -1.0)
+        rad3 = keep.tile([P, TILES], F32, name="rad3")
+
+        warm_in = keep.tile([P, 1], F32, name="warm_in")
+        warm_out = keep.tile([P, 1], F32, name="warm_out")
+        nc.vector.memset(warm_in[:], 0.0)
+        nc.scalar.activation(out=warm_out[:], in_=warm_in[:], func=ACT.Tanh)
+
+        def weight_tiles(tag):
+            grouped = keep.tile([P, F * T], BF16, name=tag + "_grp", align_bytes=64)
+            codes = keep.tile([P, F], U32, name=tag + "_codes", align_bytes=64)
+            scales = keep.tile([P, F], U8, name=tag + "_scales", align_bytes=64)
+            return grouped, codes, scales
+
+        def group_weight(raw, grouped, permuted):
+            if permuted:
+                dst = grouped[:].rearrange("p (t m j) -> p t m j", t=T, j=T)
+                src = raw[:].rearrange("p j (m t) -> p t m j", t=T)
+            else:
+                dst = grouped[:].rearrange("p (h m j) -> p h m j", h=T, j=T)
+                src = raw[:].rearrange("p j (h m) -> p h m j", h=T)
+            nc.vector.tensor_copy(out=dst[:, 0:2], in_=src[:, 0:2])
+            nc.scalar.copy(out=dst[:, 2:4], in_=src[:, 2:4])
+
+        def quantize(grouped, codes, scales):
+            nc.vector.quantize_mx(out=codes[:].bitcast(FP8X4), scales=scales[:], in_=grouped[:])
+
+        wc_t = weight_tiles("wc")
+        w1_t = weight_tiles("w1")
+        w2_t = weight_tiles("w2")
+
+        live = {}
+
+        def widen(i):
+            chunk, j = x_at[i]
+            xw = work.tile([P, D], BF16, name="xw", bufs=4)
+            nc.vector.tensor_tensor(
+                out=xw[:], in0=chunk[:, j, :].bitcast(FP8), in1=scale[:], op=ALU.mult
+            )
+            live["xw", i] = xw
+
+        def turn(i):
+            chunk, j = c_at[i]
+            xt = ps_xt.tile([P, 4, P], F32, name="xt")
+            for c, src in enumerate((live["xw", i][:], chunk[:, j, :])):
+                words = src.bitcast(F32)
+                for u in range(2):
+                    nc.tensor.transpose(xt[:, 2 * c + u, :], words[:, u::2], ident[:])
+            live["xt", i] = xt
+
+        def empty(i):
+            grp = work.tile([P, 2 * P * T], BF16, name="grp", align_bytes=64)
+            nc.scalar.copy(
+                out=grp[:].bitcast(F32).rearrange("p (c r u) -> p c r u", c=2, u=2),
+                in_=live["xt", i][:].rearrange("p (c u) r -> p c r u", c=2),
+            )
+            live["grp", i] = grp
+
+        def quant1(i):
+            xq = work.tile([P, 2 * P], U32, name="xq", align_bytes=64)
+            xs = work.tile([P, 2 * P], U8, name="xs", align_bytes=64)
+            quantize(live["grp", i], xq, xs)
+            live["xq", i] = (xq, xs)
+
+        def stage1(i):
+            xq, xs = live["xq", i]
+            a = ps_a.tile([P, T, P], F32, name="a")
+            u = ps_u.tile([P, T, P], F32, name="u")
+            for acc, w, lo in ((a, wc_t, P), (u, w1_t, 0)):
+                for t in range(T):
+                    nc.tensor.matmul_mx(
+                        out=acc[:, t, :],
+                        lhsT=w[1][:, t * P : (t + 1) * P].bitcast(FP8X4),
+                        lhsT_scale=w[2][:, t * P : (t + 1) * P],
+                        rhs=xq[:, lo : lo + P].bitcast(FP8X4),
+                        rhs_scale=xs[:, lo : lo + P],
+                        start=True,
+                        stop=True,
+                    )
+            live["a", i] = a
+            live["u", i] = u
+
+        def tanh(i):
+            th = work.tile([P, P, T], F32, name="th")
+            nc.scalar.activation(
+                out=th[:], in_=live["a", i][:].rearrange("p t r -> p r t"), func=ACT.Tanh
+            )
+            live["th", i] = th
+            live["hb", i] = work.tile([P, 2, P * T], BF16, name="hb", align_bytes=64)
+
+        def neg_u(i):
+            nc.scalar.activation(
+                out=live["hb", i][:, 1, :].rearrange("p (r t) -> p r t", t=T),
+                in_=live["u", i][:].rearrange("p t r -> p r t"),
+                func=ACT.Copy,
+                scale=-1.0,
+            )
+
+        def modulate(i):
+            nc.vector.scalar_tensor_tensor(
+                out=live["hb", i][:, 0, :].rearrange("p (r t) -> p r t", t=T),
+                in0=live["th", i][:],
+                scalar=1.0,
+                in1=live["u", i][:].rearrange("p t r -> p r t"),
+                op0=ALU.add,
+                op1=ALU.mult,
+            )
+
+        def quant2(i):
+            hq = work.tile([P, 2 * P], U32, name="hq", align_bytes=64)
+            hs = work.tile([P, 2 * P], U8, name="hs", align_bytes=64)
+            nc.vector.quantize_mx(
+                out=hq[:].bitcast(FP8X4),
+                scales=hs[:],
+                in_=live["hb", i][:].rearrange("p h n -> p (h n)"),
+            )
+            live["hq", i] = (hq, hs)
+
+        def stage2(i):
+            hq, hs = live["hq", i]
+
+            def product(acc, h, start, stop):
+                nc.tensor.matmul_mx(
+                    out=acc[:],
+                    lhsT=hq[:, h * P : (h + 1) * P].bitcast(FP8X4),
+                    lhsT_scale=hs[:, h * P : (h + 1) * P],
+                    rhs=w2_t[1][:].bitcast(FP8X4),
+                    rhs_scale=w2_t[2][:],
+                    start=start,
+                    stop=stop,
+                )
+
+            q = ps_q.tile([P, D], F32, name="q")
+            dc = ps_dc.tile([P, D], F32, name="dc")
+            product(dc, 0, True, True)
+            product(q, 0, True, False)
+            product(q, 1, False, True)
+            live["dc", i] = dc
+            live["q", i] = q
+
+        def delta(i):
+            chunk, j = d_at[i]
+            dl = work.tile([P, D], F32, name="dl", bufs=5)
+            nc.vector.scalar_tensor_tensor(
+                out=dl[:],
+                in0=chunk[:, j, :],
+                scalar=-0.5,
+                in1=live["q", i][:],
+                op0=ALU.mult,
+                op1=ALU.add,
+            )
+            live["dl", i] = dl
+
+        def sum_dc(i):
+            st = work.tile([P, 2], F32, name="st", bufs=4)
+            live["st", i] = st
+            sq = work.tile([P, D], F32, name="sq", bufs=2)
+            nc.scalar.activation(
+                out=sq[:], in_=live["dc", i][:], func=ACT.Square, accum_out=st[:, 1:2]
+            )
+
+        def sum_delta(i):
+            sq = work.tile([P, D], F32, name="sq", bufs=2)
+            nc.scalar.activation(
+                out=sq[:], in_=live["dl", i][:], func=ACT.Square, accum_out=live["st", i][:, 0:1]
+            )
+
+        def sum_cross(i):
+            pr = work.tile([P, D], F32, name="pr", bufs=2)
+            kk = work.tile([P, 1], F32, name="kk", bufs=4)
+            nc.vector.scalar_tensor_tensor(
+                out=pr[:],
+                in0=live["dc", i][:],
+                scalar=1.0,
+                in1=live["dl", i][:],
+                op0=ALU.mult,
+                op1=ALU.mult,
+                accum_out=kk[:],
+            )
+            live["kk", i] = kk
+
+        def row_scalars(i):
+            pw = work.tile([P, 2], F32, name="pw", bufs=4)
+            bb = work.tile([P, 1], F32, name="bb", bufs=4)
+            c3 = work.tile([P, 1], F32, name="c3", bufs=4)
+            aa = work.tile([P, 1], F32, name="aa", bufs=4)
+            nc.gpsimd.tensor_tensor(out=pw[:], in0=live["st", i][:], in1=expo[:], op=ALU.pow)
+            nc.gpsimd.tensor_scalar(
+                out=bb[:], in0=pw[:, 0:1], scalar1=rad3[:, i : i + 1], scalar2=3.0, op0=ALU.mult, op1=ALU.min
+            )
+            nc.gpsimd.tensor_scalar(
+                out=c3[:], in0=live["kk", i][:], scalar1=pw[:, 1:2], scalar2=bb[:], op0=ALU.mult, op1=ALU.mult
+            )
+            nc.gpsimd.tensor_scalar(
+                out=aa[:], in0=c3[:], scalar1=-1.0, scalar2=1.0, op0=ALU.mult, op1=ALU.add
+            )
+            live["ab", i] = (aa, bb)
+
+        def scale_dc(i):
+            t1 = work.tile([P, D], F32, name="t1")
+            nc.scalar.activation(
+                out=t1[:], in_=live["dc", i][:], func=ACT.Copy, scale=live["ab", i][0][:]
+            )
+            live["t1", i] = t1
+
+        def combine(i):
+            if i % 2 == 0:
+                live["ot", i // 2] = work.tile([P, 2, D], F32, name="ot", bufs=4)
+            ot = live["ot", i // 2]
+            nc.vector.scalar_tensor_tensor(
+                out=ot[:, i % 2, :],
+                in0=live["dl", i][:],
+                scalar=live["ab", i][1][:],
+                in1=live["t1", i][:],
+                op0=ALU.mult,
+                op1=ALU.add,
+            )
+            if i >= TILES - 2:
+                nc.sync.dma_start(out=ov[:, i, :], in_=ot[:, i % 2, :])
+            elif i % 2 == 1:
+                nc.sync.dma_start(out=ov[:, i - 1 : i + 1, :], in_=ot[:])
+
+        def at(stage, i):
+            if 0 <= i < TILES:
+                stage(i)
+
+        for s in range(-4, TILES + 3):
+            if s == -3:
+                group_weight(wc_raw, wc_t[0], True)
+                group_weight(w1_raw, w1_t[0], True)
+            if s == -1:
+                quantize(*wc_t)
+                quantize(*w1_t)
+                nc.gpsimd.tensor_scalar(
+                    out=rad3[:], in0=rad[:], scalar1=3.0, scalar2=0.0, op0=ALU.mult, op1=ALU.add
+                )
+            if s == 0:
+                group_weight(w2_raw, w2_t[0], False)
+            at(modulate, s)
+            at(quant1, s + 1)
+            at(stage1, s + 1)
+            at(empty, s + 2)
+            at(scale_dc, s - 3)
+            at(delta, s - 1)
+            at(tanh, s + 1)
+            at(sum_delta, s - 1)
+            at(neg_u, s + 1)
+            if s == 0:
+                quantize(*w2_t)
+            at(quant2, s)
+            at(stage2, s)
+            at(sum_cross, s - 1)
+            at(row_scalars, s - 1)
+            at(sum_dc, s)
+            at(widen, s + 4)
+            at(combine, s - 3)
+            at(turn, s + 3)

@@ -297,12 +297,12 @@ def tile_adaptiveprojectedguidancehead_t_kernel(
             )
             live["ab", i] = (aa, bb)
 
-        def scale_dc(i):
-            t1 = work.tile([P, D], F32, name="t1")
+        def scale_delta(i):
+            sd = work.tile([P, D], F32, name="sd")
             nc.scalar.activation(
-                out=t1[:], in_=live["dc", i][:], func=ACT.Copy, scale=live["ab", i][0][:]
+                out=sd[:], in_=live["dl", i][:], func=ACT.Copy, scale=live["ab", i][1][:]
             )
-            live["t1", i] = t1
+            live["sd", i] = sd
 
         def combine(i):
             if i % 2 == 0:
@@ -310,9 +310,9 @@ def tile_adaptiveprojectedguidancehead_t_kernel(
             ot = live["ot", i // 2]
             nc.vector.scalar_tensor_tensor(
                 out=ot[:, i % 2, :],
-                in0=live["dl", i][:],
-                scalar=live["ab", i][1][:],
-                in1=live["t1", i][:],
+                in0=live["dc", i][:],
+                scalar=live["ab", i][0][:],
+                in1=live["sd", i][:],
                 op0=ALU.mult,
                 op1=ALU.add,
             )
@@ -325,34 +325,33 @@ def tile_adaptiveprojectedguidancehead_t_kernel(
             if 0 <= i < TILES:
                 stage(i)
 
-        for s in range(-4, TILES + 3):
-            if s == -3:
-                group_weight(wc_raw, wc_t[0], True)
-                group_weight(w1_raw, w1_t[0], True)
-            if s == -1:
+        for s in range(-4, TILES + 2):
+            if s == -2:
                 quantize(*wc_t)
                 quantize(*w1_t)
+                group_weight(w2_raw, w2_t[0], False)
                 nc.gpsimd.tensor_scalar(
                     out=rad3[:], in0=rad[:], scalar1=3.0, scalar2=0.0, op0=ALU.mult, op1=ALU.add
                 )
-            if s == 0:
-                group_weight(w2_raw, w2_t[0], False)
-            at(modulate, s)
-            at(quant1, s + 1)
-            at(stage1, s + 1)
-            at(empty, s + 2)
-            at(scale_dc, s - 3)
-            at(delta, s - 1)
             at(tanh, s + 1)
-            at(sum_delta, s - 1)
             at(neg_u, s + 1)
-            if s == 0:
-                quantize(*w2_t)
-            at(quant2, s)
-            at(stage2, s)
+            at(sum_dc, s)
+            at(turn, s + 3)
+            at(empty, s + 3)
             at(sum_cross, s - 1)
             at(row_scalars, s - 1)
-            at(sum_dc, s)
+            at(combine, s - 2)
+            at(quant1, s + 2)
+            at(stage1, s + 2)
+            at(delta, s)
+            at(sum_delta, s)
+            at(scale_delta, s - 1)
+            at(modulate, s + 1)
             at(widen, s + 4)
-            at(combine, s - 3)
-            at(turn, s + 3)
+            if s == -4:
+                group_weight(wc_raw, wc_t[0], True)
+                group_weight(w1_raw, w1_t[0], True)
+            if s == -1:
+                quantize(*w2_t)
+            at(quant2, s + 1)
+            at(stage2, s + 1)

@@ -32,9 +32,9 @@ def tile_adaptiveprojectedguidancehead_t_kernel(
         keep = ctx.enter_context(tc.tile_pool(name="keep", bufs=1))
         work = ctx.enter_context(tc.tile_pool(name="work", bufs=3))
         ps_xt = ctx.enter_context(tc.psum_pool(name="ps_xt", bufs=1))
-        ps_u = ctx.enter_context(tc.psum_pool(name="ps_u", bufs=2))
+        ps_u = ctx.enter_context(tc.psum_pool(name="ps_u", bufs=1))
         ps_a = ctx.enter_context(tc.psum_pool(name="ps_a", bufs=1))
-        ps_dc = ctx.enter_context(tc.psum_pool(name="ps_dc", bufs=3))
+        ps_dc = ctx.enter_context(tc.psum_pool(name="ps_dc", bufs=4))
         ps_q = ctx.enter_context(tc.psum_pool(name="ps_q", bufs=1))
 
         xv = x_bytes.rearrange("(p i) k -> p i k", i=TILES)
@@ -72,12 +72,14 @@ def tile_adaptiveprojectedguidancehead_t_kernel(
         scale = keep.tile([P, D], F32, name="scale")
         rad = keep.tile([P, TILES], BF16, name="rad")
 
-        load(c_chunks, cv, 0)
+        scale_row = keep.tile([P, D], F32, name="scale_row")
+        ones = keep.tile([P, P], F32, name="ones")
+        nc.gpsimd.memset(scale_row[:], 0.0)
+        nc.gpsimd.memset(ones[:], 1.0)
+        nc.sync.dma_start(out=scale_row[0:1, :], in_=x_scale)
         load(x_chunks, xv, 0)
+        load(c_chunks, cv, 0)
         wc_raw = load_weight(wc, "wc")
-        nc.sync.dma_start(
-            out=scale[:], in_=x_scale.rearrange("o k -> (o k)").partition_broadcast(P)
-        )
         w1_raw = load_weight(w1, "w1")
         load(c_chunks, cv, 1)
         load(x_chunks, xv, 1)
@@ -132,6 +134,11 @@ def tile_adaptiveprojectedguidancehead_t_kernel(
 
         live = {}
 
+        def spread_scale():
+            bank = ps_q.tile([P, D], F32, name="q")
+            nc.tensor.matmul(bank[:], lhsT=ones[:], rhs=scale_row[:], start=True, stop=True)
+            nc.scalar.copy(out=scale[:], in_=bank[:])
+
         def widen(i):
             chunk, j = x_at[i]
             xw = work.tile([P, D], BF16, name="xw", bufs=4)
@@ -148,6 +155,16 @@ def tile_adaptiveprojectedguidancehead_t_kernel(
                 for u in range(2):
                     nc.tensor.transpose(xt[:, 2 * c + u, :], words[:, u::2], ident[:])
             live["xt", i] = xt
+            if i >= 1:
+                live["a", i - 1] = ps_a.tile([P, T, P], F32, name="a")
+            if i >= 3:
+                nc.tensor.matmul(
+                    live["a", i - 1][:].rearrange("p t r -> p (t r)"),
+                    lhsT=wc_t[0][:, :P],
+                    rhs=wc_t[0][:, : T * P],
+                    start=True,
+                    stop=True,
+                )
 
         def empty(i):
             grp = work.tile([P, 2 * P * T], BF16, name="grp", align_bytes=64)
@@ -165,7 +182,9 @@ def tile_adaptiveprojectedguidancehead_t_kernel(
 
         def stage1(i):
             xq, xs = live["xq", i]
-            a = ps_a.tile([P, T, P], F32, name="a")
+            if i == TILES - 1:
+                live["a", i] = ps_a.tile([P, T, P], F32, name="a")
+            a = live["a", i]
             u = ps_u.tile([P, T, P], F32, name="u")
             for acc, w, lo in ((a, wc_t, P), (u, w1_t, 0)):
                 for t in range(T):
@@ -178,7 +197,6 @@ def tile_adaptiveprojectedguidancehead_t_kernel(
                         start=True,
                         stop=True,
                     )
-            live["a", i] = a
             live["u", i] = u
 
         def tanh(i):
@@ -253,7 +271,7 @@ def tile_adaptiveprojectedguidancehead_t_kernel(
             live["dl", i] = dl
 
         def sum_dc(i):
-            st = work.tile([P, 2], F32, name="st", bufs=4)
+            st = work.tile([P, 2], F32, name="st", bufs=5)
             live["st", i] = st
             sq = work.tile([P, D], F32, name="sq", bufs=2)
             nc.scalar.activation(
@@ -280,27 +298,41 @@ def tile_adaptiveprojectedguidancehead_t_kernel(
             )
             live["kk", i] = kk
 
-        def row_scalars(i):
-            pw = work.tile([P, 2], F32, name="pw", bufs=4)
-            bb = work.tile([P, 1], F32, name="bb", bufs=4)
-            c3 = work.tile([P, 1], F32, name="c3", bufs=4)
-            aa = work.tile([P, 1], F32, name="aa", bufs=4)
+        def powers(i):
+            pw = work.tile([P, 2], F32, name="pw", bufs=5)
             nc.gpsimd.tensor_tensor(out=pw[:], in0=live["st", i][:], in1=expo[:], op=ALU.pow)
-            nc.gpsimd.tensor_scalar(
-                out=bb[:], in0=pw[:, 0:1], scalar1=rad3[:, i : i + 1], scalar2=3.0, op0=ALU.mult, op1=ALU.min
+            live["pw", i] = pw
+
+        def neg_step(i):
+            nb = work.tile([P, 1], F32, name="nb", bufs=5)
+            nc.vector.tensor_scalar(
+                out=nb[:],
+                in0=live["pw", i][:, 0:1],
+                scalar1=rad3[:, i : i + 1],
+                scalar2=-3.0,
+                op0=ALU.mult,
+                op1=ALU.max,
             )
-            nc.gpsimd.tensor_scalar(
-                out=c3[:], in0=live["kk", i][:], scalar1=pw[:, 1:2], scalar2=bb[:], op0=ALU.mult, op1=ALU.mult
+            live["nb", i] = nb
+
+        def ratio(i):
+            ka = work.tile([P, 1], F32, name="ka", bufs=5)
+            nc.scalar.activation(
+                out=ka[:], in_=live["kk", i][:], func=ACT.Copy, scale=live["pw", i][:, 1:2]
             )
-            nc.gpsimd.tensor_scalar(
-                out=aa[:], in0=c3[:], scalar1=-1.0, scalar2=1.0, op0=ALU.mult, op1=ALU.add
+            live["ka", i] = ka
+
+        def keep_dc(i):
+            aa = work.tile([P, 1], F32, name="aa", bufs=5)
+            nc.scalar.activation(
+                out=aa[:], in_=live["ka", i][:], func=ACT.Identity, scale=live["nb", i][:], bias=1.0
             )
-            live["ab", i] = (aa, bb)
+            live["aa", i] = aa
 
         def scale_delta(i):
             sd = work.tile([P, D], F32, name="sd")
             nc.scalar.activation(
-                out=sd[:], in_=live["dl", i][:], func=ACT.Copy, scale=live["ab", i][1][:]
+                out=sd[:], in_=live["dl", i][:], func=ACT.Copy, scale=live["nb", i][:]
             )
             live["sd", i] = sd
 
@@ -311,10 +343,10 @@ def tile_adaptiveprojectedguidancehead_t_kernel(
             nc.vector.scalar_tensor_tensor(
                 out=ot[:, i % 2, :],
                 in0=live["dc", i][:],
-                scalar=live["ab", i][0][:],
+                scalar=live["aa", i][:],
                 in1=live["sd", i][:],
                 op0=ALU.mult,
-                op1=ALU.add,
+                op1=ALU.subtract,
             )
             if i >= TILES - 2:
                 nc.sync.dma_start(out=ov[:, i, :], in_=ot[:, i % 2, :])
@@ -325,31 +357,36 @@ def tile_adaptiveprojectedguidancehead_t_kernel(
             if 0 <= i < TILES:
                 stage(i)
 
-        for s in range(-4, TILES + 2):
+        spread_scale()
+        for s in range(-4, TILES + 3):
             if s == -2:
                 quantize(*wc_t)
                 quantize(*w1_t)
                 group_weight(w2_raw, w2_t[0], False)
                 nc.gpsimd.tensor_scalar(
-                    out=rad3[:], in0=rad[:], scalar1=3.0, scalar2=0.0, op0=ALU.mult, op1=ALU.add
+                    out=rad3[:], in0=rad[:], scalar1=-3.0, scalar2=0.0, op0=ALU.mult, op1=ALU.add
                 )
             at(tanh, s + 1)
+            at(ratio, s - 2)
             at(neg_u, s + 1)
+            at(keep_dc, s - 2)
             at(sum_dc, s)
+            at(scale_delta, s - 2)
             at(turn, s + 3)
             at(empty, s + 3)
             at(sum_cross, s - 1)
-            at(row_scalars, s - 1)
-            at(combine, s - 2)
-            at(quant1, s + 2)
-            at(stage1, s + 2)
+            at(powers, s - 1)
+            at(combine, s - 3)
+            at(modulate, s + 1)
+            at(neg_step, s - 1)
             at(delta, s)
             at(sum_delta, s)
-            at(scale_delta, s - 1)
-            at(modulate, s + 1)
-            at(widen, s + 4)
+            at(quant1, s + 2)
+            at(stage1, s + 2)
             if s == -4:
                 group_weight(wc_raw, wc_t[0], True)
+            at(widen, s + 4)
+            if s == -4:
                 group_weight(w1_raw, w1_t[0], True)
             if s == -1:
                 quantize(*w2_t)

@@ -31,10 +31,11 @@ def tile_adaptiveprojectedguidancehead_t_kernel(
     with ExitStack() as ctx:
         keep = ctx.enter_context(tc.tile_pool(name="keep", bufs=1))
         work = ctx.enter_context(tc.tile_pool(name="work", bufs=3))
-        ps_xt = ctx.enter_context(tc.psum_pool(name="ps_xt", bufs=1))
+        ps_xx = ctx.enter_context(tc.psum_pool(name="ps_xx", bufs=1))
+        ps_xc = ctx.enter_context(tc.psum_pool(name="ps_xc", bufs=1))
         ps_u = ctx.enter_context(tc.psum_pool(name="ps_u", bufs=1))
         ps_a = ctx.enter_context(tc.psum_pool(name="ps_a", bufs=1))
-        ps_dc = ctx.enter_context(tc.psum_pool(name="ps_dc", bufs=4))
+        ps_dc = ctx.enter_context(tc.psum_pool(name="ps_dc", bufs=3))
         ps_q = ctx.enter_context(tc.psum_pool(name="ps_q", bufs=1))
 
         xv = x_bytes.rearrange("(p i) k -> p i k", i=TILES)
@@ -69,17 +70,13 @@ def tile_adaptiveprojectedguidancehead_t_kernel(
             nc.sync.dma_start(out=raw[:], in_=w.rearrange("(p j) n -> p j n", j=T))
             return raw
 
-        scale = keep.tile([P, D], F32, name="scale")
+        scale = keep.tile([P, T], F32, name="scale")
         rad = keep.tile([P, TILES], BF16, name="rad")
 
-        scale_row = keep.tile([P, D], F32, name="scale_row")
-        ones = keep.tile([P, P], F32, name="ones")
-        nc.gpsimd.memset(scale_row[:], 0.0)
-        nc.gpsimd.memset(ones[:], 1.0)
-        nc.sync.dma_start(out=scale_row[0:1, :], in_=x_scale)
         load(x_chunks, xv, 0)
         load(c_chunks, cv, 0)
         wc_raw = load_weight(wc, "wc")
+        nc.sync.dma_start(out=scale[:], in_=x_scale.rearrange("o (p t) -> p (o t)", t=T))
         w1_raw = load_weight(w1, "w1")
         load(c_chunks, cv, 1)
         load(x_chunks, xv, 1)
@@ -134,57 +131,52 @@ def tile_adaptiveprojectedguidancehead_t_kernel(
 
         live = {}
 
-        def spread_scale():
-            bank = ps_q.tile([P, D], F32, name="q")
-            nc.tensor.matmul(bank[:], lhsT=ones[:], rhs=scale_row[:], start=True, stop=True)
-            nc.scalar.copy(out=scale[:], in_=bank[:])
-
         def widen(i):
             chunk, j = x_at[i]
             xw = work.tile([P, D], BF16, name="xw", bufs=4)
-            nc.vector.tensor_tensor(
-                out=xw[:], in0=chunk[:, j, :].bitcast(FP8), in1=scale[:], op=ALU.mult
-            )
+            nc.scalar.copy(out=xw[:], in_=chunk[:, j, :].bitcast(FP8))
             live["xw", i] = xw
 
         def turn(i):
             chunk, j = c_at[i]
-            xt = ps_xt.tile([P, 4, P], F32, name="xt")
-            for c, src in enumerate((live["xw", i][:], chunk[:, j, :])):
-                words = src.bitcast(F32)
+            xx = ps_xx.tile([P, 2, P], F32, name="xx")
+            xc = ps_xc.tile([P, 2, P], F32, name="xc")
+            for turned, rows in ((xx, live["xw", i][:]), (xc, chunk[:, j, :])):
+                words = rows.bitcast(F32)
                 for u in range(2):
-                    nc.tensor.transpose(xt[:, 2 * c + u, :], words[:, u::2], ident[:])
-            live["xt", i] = xt
-            if i >= 1:
-                live["a", i - 1] = ps_a.tile([P, T, P], F32, name="a")
-            if i >= 3:
-                nc.tensor.matmul(
-                    live["a", i - 1][:].rearrange("p t r -> p (t r)"),
-                    lhsT=wc_t[0][:, :P],
-                    rhs=wc_t[0][:, : T * P],
-                    start=True,
-                    stop=True,
-                )
+                    nc.tensor.transpose(turned[:, u, :], words[:, u::2], ident[:])
+            live["xx", i] = xx
+            live["xc", i] = xc
+
+        def scale_x(i):
+            nc.vector.tensor_tensor(
+                out=live["grp", i][:, 0, :].rearrange("p (r u e) -> p r u e", u=2, e=2),
+                in0=live["xx", i][:].bitcast(BF16).rearrange("p u (r e) -> p r u e", e=2),
+                in1=scale[:].rearrange("p (o u e) -> p o u e", o=1, u=2).to_broadcast([P, P, 2, 2]),
+                op=ALU.mult,
+            )
 
         def empty(i):
-            grp = work.tile([P, 2 * P * T], BF16, name="grp", align_bytes=64)
+            live["grp", i] = work.tile([P, 2, P * T], BF16, name="grp", align_bytes=64)
             nc.scalar.copy(
-                out=grp[:].bitcast(F32).rearrange("p (c r u) -> p c r u", c=2, u=2),
-                in_=live["xt", i][:].rearrange("p (c u) r -> p c r u", c=2),
+                out=live["grp", i][:, 1, :].bitcast(F32).rearrange("p (r u) -> p r u", u=2),
+                in_=live["xc", i][:].rearrange("p u r -> p r u"),
             )
-            live["grp", i] = grp
 
         def quant1(i):
             xq = work.tile([P, 2 * P], U32, name="xq", align_bytes=64)
             xs = work.tile([P, 2 * P], U8, name="xs", align_bytes=64)
-            quantize(live["grp", i], xq, xs)
+            nc.vector.quantize_mx(
+                out=xq[:].bitcast(FP8X4),
+                scales=xs[:],
+                in_=live["grp", i][:].rearrange("p h n -> p (h n)"),
+            )
             live["xq", i] = (xq, xs)
 
         def stage1(i):
             xq, xs = live["xq", i]
-            if i == TILES - 1:
-                live["a", i] = ps_a.tile([P, T, P], F32, name="a")
-            a = live["a", i]
+            a = ps_a.tile([P, T, P], F32, name="a")
+            live["a", i] = a
             u = ps_u.tile([P, T, P], F32, name="u")
             for acc, w, lo in ((a, wc_t, P), (u, w1_t, 0)):
                 for t in range(T):
@@ -298,22 +290,25 @@ def tile_adaptiveprojectedguidancehead_t_kernel(
             )
             live["kk", i] = kk
 
-        def powers(i):
+        def steps(i):
             pw = work.tile([P, 2], F32, name="pw", bufs=5)
-            nc.gpsimd.tensor_tensor(out=pw[:], in0=live["st", i][:], in1=expo[:], op=ALU.pow)
-            live["pw", i] = pw
-
-        def neg_step(i):
             nb = work.tile([P, 1], F32, name="nb", bufs=5)
-            nc.vector.tensor_scalar(
+            sd = work.tile([P, D], F32, name="sd")
+            nc.gpsimd.tensor_tensor(out=pw[:], in0=live["st", i][:], in1=expo[:], op=ALU.pow)
+            nc.gpsimd.tensor_scalar(
                 out=nb[:],
-                in0=live["pw", i][:, 0:1],
+                in0=pw[:, 0:1],
                 scalar1=rad3[:, i : i + 1],
                 scalar2=-3.0,
                 op0=ALU.mult,
                 op1=ALU.max,
             )
+            nc.gpsimd.tensor_scalar(
+                out=sd[:], in0=live["dl", i][:], scalar1=nb[:], scalar2=0.0, op0=ALU.mult, op1=ALU.add
+            )
+            live["pw", i] = pw
             live["nb", i] = nb
+            live["sd", i] = sd
 
         def ratio(i):
             ka = work.tile([P, 1], F32, name="ka", bufs=5)
@@ -328,13 +323,6 @@ def tile_adaptiveprojectedguidancehead_t_kernel(
                 out=aa[:], in_=live["ka", i][:], func=ACT.Identity, scale=live["nb", i][:], bias=1.0
             )
             live["aa", i] = aa
-
-        def scale_delta(i):
-            sd = work.tile([P, D], F32, name="sd")
-            nc.scalar.activation(
-                out=sd[:], in_=live["dl", i][:], func=ACT.Copy, scale=live["nb", i][:]
-            )
-            live["sd", i] = sd
 
         def combine(i):
             if i % 2 == 0:
@@ -357,8 +345,10 @@ def tile_adaptiveprojectedguidancehead_t_kernel(
             if 0 <= i < TILES:
                 stage(i)
 
-        spread_scale()
         for s in range(-4, TILES + 3):
+            if s == -4:
+                group_weight(wc_raw, wc_t[0], True)
+                group_weight(w1_raw, w1_t[0], True)
             if s == -2:
                 quantize(*wc_t)
                 quantize(*w1_t)
@@ -366,29 +356,24 @@ def tile_adaptiveprojectedguidancehead_t_kernel(
                 nc.gpsimd.tensor_scalar(
                     out=rad3[:], in0=rad[:], scalar1=-3.0, scalar2=0.0, op0=ALU.mult, op1=ALU.add
                 )
+            at(sum_delta, s - 2)
+            at(empty, s + 2)
+            at(sum_dc, s - 1)
+            at(sum_cross, s - 2)
+            at(steps, s - 2)
+            at(modulate, s)
+            at(stage1, s + 1)
             at(tanh, s + 1)
-            at(ratio, s - 2)
             at(neg_u, s + 1)
-            at(keep_dc, s - 2)
-            at(sum_dc, s)
-            at(scale_delta, s - 2)
-            at(turn, s + 3)
-            at(empty, s + 3)
-            at(sum_cross, s - 1)
-            at(powers, s - 1)
+            at(scale_x, s + 2)
             at(combine, s - 3)
-            at(modulate, s + 1)
-            at(neg_step, s - 1)
-            at(delta, s)
-            at(sum_delta, s)
-            at(quant1, s + 2)
-            at(stage1, s + 2)
-            if s == -4:
-                group_weight(wc_raw, wc_t[0], True)
+            at(turn, s + 3)
+            at(ratio, s - 2)
             at(widen, s + 4)
-            if s == -4:
-                group_weight(w1_raw, w1_t[0], True)
+            at(keep_dc, s - 2)
+            at(delta, s - 1)
             if s == -1:
                 quantize(*w2_t)
-            at(quant2, s + 1)
-            at(stage2, s + 1)
+            at(quant2, s)
+            at(stage2, s)
+            at(quant1, s + 2)

@@ -19,7 +19,7 @@ P = 128
 T = 4
 TILES = N // P
 
-X_CHUNKS = (1, 1, 2, 4, 8, 8, 8)
+X_CHUNKS = (4, 4, 8, 8, 8)
 C_CHUNKS = (1, 1, 2, 4, 8, 8, 8)
 DP_CHUNKS = (2, 2, 4, 8, 8, 8)
 
@@ -75,23 +75,21 @@ def tile_adaptiveprojectedguidancehead_t_kernel(
 
         load(x_chunks, xv, 0)
         load(c_chunks, cv, 0)
-        wc_raw = load_weight(wc, "wc")
         nc.sync.dma_start(out=scale[:], in_=x_scale.rearrange("o (p t) -> p (o t)", t=T))
+        wc_raw = load_weight(wc, "wc")
         w1_raw = load_weight(w1, "w1")
         load(c_chunks, cv, 1)
-        load(x_chunks, xv, 1)
         w2_raw = load_weight(w2, "w2")
         load(c_chunks, cv, 2)
-        load(x_chunks, xv, 2)
         load(d_chunks, dv, 0)
         nc.sync.dma_start(out=rad[:], in_=radius.rearrange("(p i) -> p i", i=TILES))
         load(c_chunks, cv, 3)
-        load(x_chunks, xv, 3)
+        load(x_chunks, xv, 1)
         load(d_chunks, dv, 1)
         load(d_chunks, dv, 2)
         for n in range(4, 7):
             load(c_chunks, cv, n)
-            load(x_chunks, xv, n)
+            load(x_chunks, xv, n - 2)
             load(d_chunks, dv, n - 1)
 
         ident = keep.tile([P, P], F32, name="ident")
@@ -119,8 +117,13 @@ def tile_adaptiveprojectedguidancehead_t_kernel(
             else:
                 dst = grouped[:].rearrange("p (h m j) -> p h m j", h=T, j=T)
                 src = raw[:].rearrange("p j (h m) -> p h m j", h=T)
-            nc.vector.tensor_copy(out=dst[:, 0:2], in_=src[:, 0:2])
-            nc.scalar.copy(out=dst[:, 2:4], in_=src[:, 2:4])
+            return dst, src
+
+        def group_on_v(pair, lo, hi):
+            nc.vector.tensor_copy(out=pair[0][:, :, lo:hi], in_=pair[1][:, :, lo:hi])
+
+        def group_on_s(pair, lo, hi):
+            nc.scalar.copy(out=pair[0][:, :, lo:hi], in_=pair[1][:, :, lo:hi])
 
         def quantize(grouped, codes, scales):
             nc.vector.quantize_mx(out=codes[:].bitcast(FP8X4), scales=scales[:], in_=grouped[:])
@@ -150,31 +153,37 @@ def tile_adaptiveprojectedguidancehead_t_kernel(
 
         def scale_x(i):
             nc.vector.tensor_tensor(
-                out=live["grp", i][:, 0, :].rearrange("p (r u e) -> p r u e", u=2, e=2),
+                out=live["gh", i - 2][:, 0, :].rearrange("p (r u e) -> p r u e", u=2, e=2),
                 in0=live["xx", i][:].bitcast(BF16).rearrange("p u (r e) -> p r u e", e=2),
                 in1=scale[:].rearrange("p (o u e) -> p o u e", o=1, u=2).to_broadcast([P, P, 2, 2]),
                 op=ALU.mult,
             )
 
         def empty(i):
-            live["grp", i] = work.tile([P, 2, P * T], BF16, name="grp", align_bytes=64)
             nc.scalar.copy(
-                out=live["grp", i][:, 1, :].bitcast(F32).rearrange("p (r u) -> p r u", u=2),
+                out=live["gh", i - 2][:, 1, :].bitcast(F32).rearrange("p (r u) -> p r u", u=2),
                 in_=live["xc", i][:].rearrange("p u r -> p r u"),
             )
 
-        def quant1(i):
-            xq = work.tile([P, 2 * P], U32, name="xq", align_bytes=64)
-            xs = work.tile([P, 2 * P], U8, name="xs", align_bytes=64)
+        def quant(s):
+            front = 0 <= s + 2 < TILES
+            back = 0 <= s < TILES
+            lo = 0 if front else 2
+            hi = 4 if back else 2
+            codes = work.tile([P, 4 * P], U32, name="codes", align_bytes=64)
+            scales = work.tile([P, 4 * P], U8, name="scales", align_bytes=64)
             nc.vector.quantize_mx(
-                out=xq[:].bitcast(FP8X4),
-                scales=xs[:],
-                in_=live["grp", i][:].rearrange("p h n -> p (h n)"),
+                out=codes[:, lo * P : hi * P].bitcast(FP8X4),
+                scales=scales[:, lo * P : hi * P],
+                in_=live["gh", s][:, lo:hi, :].rearrange("p h n -> p (h n)"),
             )
-            live["xq", i] = (xq, xs)
+            live["codes", s] = (codes, scales)
+
+        def new_gh(s):
+            live["gh", s] = work.tile([P, 4, P * T], BF16, name="gh", align_bytes=64)
 
         def stage1(i):
-            xq, xs = live["xq", i]
+            xq, xs = live["codes", i - 2]
             a = ps_a.tile([P, T, P], F32, name="a")
             live["a", i] = a
             u = ps_u.tile([P, T, P], F32, name="u")
@@ -197,11 +206,10 @@ def tile_adaptiveprojectedguidancehead_t_kernel(
                 out=th[:], in_=live["a", i][:].rearrange("p t r -> p r t"), func=ACT.Tanh
             )
             live["th", i] = th
-            live["hb", i] = work.tile([P, 2, P * T], BF16, name="hb", align_bytes=64)
 
         def neg_u(i):
             nc.scalar.activation(
-                out=live["hb", i][:, 1, :].rearrange("p (r t) -> p r t", t=T),
+                out=live["gh", i][:, 3, :].rearrange("p (r t) -> p r t", t=T),
                 in_=live["u", i][:].rearrange("p t r -> p r t"),
                 func=ACT.Copy,
                 scale=-1.0,
@@ -209,7 +217,7 @@ def tile_adaptiveprojectedguidancehead_t_kernel(
 
         def modulate(i):
             nc.vector.scalar_tensor_tensor(
-                out=live["hb", i][:, 0, :].rearrange("p (r t) -> p r t", t=T),
+                out=live["gh", i][:, 2, :].rearrange("p (r t) -> p r t", t=T),
                 in0=live["th", i][:],
                 scalar=1.0,
                 in1=live["u", i][:].rearrange("p t r -> p r t"),
@@ -217,18 +225,8 @@ def tile_adaptiveprojectedguidancehead_t_kernel(
                 op1=ALU.mult,
             )
 
-        def quant2(i):
-            hq = work.tile([P, 2 * P], U32, name="hq", align_bytes=64)
-            hs = work.tile([P, 2 * P], U8, name="hs", align_bytes=64)
-            nc.vector.quantize_mx(
-                out=hq[:].bitcast(FP8X4),
-                scales=hs[:],
-                in_=live["hb", i][:].rearrange("p h n -> p (h n)"),
-            )
-            live["hq", i] = (hq, hs)
-
         def stage2(i):
-            hq, hs = live["hq", i]
+            hq, hs = live["codes", i]
 
             def product(acc, h, start, stop):
                 nc.tensor.matmul_mx(
@@ -243,9 +241,9 @@ def tile_adaptiveprojectedguidancehead_t_kernel(
 
             q = ps_q.tile([P, D], F32, name="q")
             dc = ps_dc.tile([P, D], F32, name="dc")
-            product(dc, 0, True, True)
-            product(q, 0, True, False)
-            product(q, 1, False, True)
+            product(dc, 2, True, True)
+            product(q, 2, True, False)
+            product(q, 3, False, True)
             live["dc", i] = dc
             live["q", i] = q
 
@@ -282,7 +280,7 @@ def tile_adaptiveprojectedguidancehead_t_kernel(
             nc.vector.scalar_tensor_tensor(
                 out=pr[:],
                 in0=live["dc", i][:],
-                scalar=1.0,
+                scalar=live["pw", i][:, 1:2],
                 in1=live["dl", i][:],
                 op0=ALU.mult,
                 op1=ALU.mult,
@@ -303,40 +301,51 @@ def tile_adaptiveprojectedguidancehead_t_kernel(
                 op0=ALU.mult,
                 op1=ALU.max,
             )
-            nc.gpsimd.tensor_scalar(
-                out=sd[:], in0=live["dl", i][:], scalar1=nb[:], scalar2=0.0, op0=ALU.mult, op1=ALU.add
-            )
+            if i < TILES - 1:
+                nc.gpsimd.tensor_scalar(
+                    out=sd[:], in0=live["dl", i][:], scalar1=nb[:], scalar2=0.0, op0=ALU.mult, op1=ALU.add
+                )
             live["pw", i] = pw
             live["nb", i] = nb
             live["sd", i] = sd
 
-        def ratio(i):
-            ka = work.tile([P, 1], F32, name="ka", bufs=5)
-            nc.scalar.activation(
-                out=ka[:], in_=live["kk", i][:], func=ACT.Copy, scale=live["pw", i][:, 1:2]
-            )
-            live["ka", i] = ka
-
         def keep_dc(i):
             aa = work.tile([P, 1], F32, name="aa", bufs=5)
             nc.scalar.activation(
-                out=aa[:], in_=live["ka", i][:], func=ACT.Identity, scale=live["nb", i][:], bias=1.0
+                out=aa[:], in_=live["kk", i][:], func=ACT.Identity, scale=live["nb", i][:], bias=1.0
             )
             live["aa", i] = aa
+
+        def combine_columns(i, ot, cols):
+            nc.vector.scalar_tensor_tensor(
+                out=ot[:, i % 2, cols],
+                in0=live["dc", i][:, cols],
+                scalar=live["aa", i][:],
+                in1=live["sd", i][:, cols],
+                op0=ALU.mult,
+                op1=ALU.subtract,
+            )
 
         def combine(i):
             if i % 2 == 0:
                 live["ot", i // 2] = work.tile([P, 2, D], F32, name="ot", bufs=4)
             ot = live["ot", i // 2]
-            nc.vector.scalar_tensor_tensor(
-                out=ot[:, i % 2, :],
-                in0=live["dc", i][:],
-                scalar=live["aa", i][:],
-                in1=live["sd", i][:],
-                op0=ALU.mult,
-                op1=ALU.subtract,
-            )
-            if i >= TILES - 2:
+            if i == TILES - 1:
+                halves = (slice(0, D // 2), slice(D // 2, D))
+                for cols in halves:
+                    nc.vector.tensor_scalar(
+                        out=live["sd", i][:, cols],
+                        in0=live["dl", i][:, cols],
+                        scalar1=live["nb", i][:],
+                        scalar2=None,
+                        op0=ALU.mult,
+                    )
+                for cols in halves:
+                    combine_columns(i, ot, cols)
+                    nc.sync.dma_start(out=ov[:, i, cols], in_=ot[:, i % 2, cols])
+                return
+            combine_columns(i, ot, slice(0, D))
+            if i == TILES - 2:
                 nc.sync.dma_start(out=ov[:, i, :], in_=ot[:, i % 2, :])
             elif i % 2 == 1:
                 nc.sync.dma_start(out=ov[:, i - 1 : i + 1, :], in_=ot[:])
@@ -345,35 +354,57 @@ def tile_adaptiveprojectedguidancehead_t_kernel(
             if 0 <= i < TILES:
                 stage(i)
 
-        for s in range(-4, TILES + 3):
-            if s == -4:
-                group_weight(wc_raw, wc_t[0], True)
-                group_weight(w1_raw, w1_t[0], True)
-            if s == -2:
-                quantize(*wc_t)
-                quantize(*w1_t)
-                group_weight(w2_raw, w2_t[0], False)
-                nc.gpsimd.tensor_scalar(
-                    out=rad3[:], in0=rad[:], scalar1=-3.0, scalar2=0.0, op0=ALU.mult, op1=ALU.add
-                )
-            at(sum_delta, s - 2)
+        wc_pair = group_weight(wc_raw, wc_t[0], True)
+        w1_pair = group_weight(w1_raw, w1_t[0], True)
+        w2_pair = group_weight(w2_raw, w2_t[0], False)
+        widen(0)
+        turn(0)
+        widen(1)
+        group_on_v(wc_pair, 0, 96)
+        group_on_s(wc_pair, 96, P)
+        new_gh(-2)
+        scale_x(0)
+        empty(0)
+        group_on_v(w1_pair, 0, 96)
+        group_on_s(w1_pair, 96, P)
+        turn(1)
+        widen(2)
+        quant(-2)
+        quantize(*wc_t)
+        quantize(*w1_t)
+        stage1(0)
+        group_on_s(w2_pair, 32, P)
+        new_gh(-1)
+        scale_x(1)
+        empty(1)
+        new_gh(0)
+        tanh(0)
+        neg_u(0)
+        turn(2)
+        widen(3)
+        group_on_v(w2_pair, 0, 32)
+        quant(-1)
+        quantize(*w2_t)
+        nc.gpsimd.tensor_scalar(
+            out=rad3[:], in0=rad[:], scalar1=-3.0, scalar2=0.0, op0=ALU.mult, op1=ALU.add
+        )
+        for s in range(TILES + 3):
             at(empty, s + 2)
             at(sum_dc, s - 1)
-            at(sum_cross, s - 2)
             at(steps, s - 2)
+            new_gh(s + 1)
             at(modulate, s)
             at(stage1, s + 1)
             at(tanh, s + 1)
             at(neg_u, s + 1)
             at(scale_x, s + 2)
             at(combine, s - 3)
+            at(delta, s - 1)
+            if s < TILES:
+                quant(s)
+            at(sum_cross, s - 2)
+            at(sum_delta, s - 1)
             at(turn, s + 3)
-            at(ratio, s - 2)
             at(widen, s + 4)
             at(keep_dc, s - 2)
-            at(delta, s - 1)
-            if s == -1:
-                quantize(*w2_t)
-            at(quant2, s)
             at(stage2, s)
-            at(quant1, s + 2)

from contextlib import ExitStack

import concourse.mybir as mybir
from concourse.masks import make_identity

N, D, C, F = 4096, 512, 512, 512
FLOPS = 4 * 2 * N * D * F

F32 = mybir.dt.float32
BF16 = mybir.dt.bfloat16
U32 = mybir.dt.uint32
U8 = mybir.dt.uint8
FP8 = mybir.dt.float8_e4m3fn
FP8X4 = mybir.dt.float8_e4m3fn_x4
ALU = mybir.AluOpType
ACT = mybir.ActivationFunctionType

P = 128
T = 4
TILES = N // P

X_CHUNKS = (4, 4, 8, 8, 8)
C_CHUNKS = (1, 1, 2, 4, 8, 8, 8)
DP_CHUNKS = (2, 2, 4, 8, 8, 8)


def tile_adaptiveprojectedguidancehead_t_kernel(
    tc, x_bytes, x_scale, cond, w1, wc, w2, delta_prev, radius, out
):
    nc = tc.nc
    with ExitStack() as ctx:
        keep = ctx.enter_context(tc.tile_pool(name="keep", bufs=1))
        work = ctx.enter_context(tc.tile_pool(name="work", bufs=3))
        ps_xx = ctx.enter_context(tc.psum_pool(name="ps_xx", bufs=1))
        ps_xc = ctx.enter_context(tc.psum_pool(name="ps_xc", bufs=1))
        ps_u = ctx.enter_context(tc.psum_pool(name="ps_u", bufs=1))
        ps_a = ctx.enter_context(tc.psum_pool(name="ps_a", bufs=1))
        ps_dc = ctx.enter_context(tc.psum_pool(name="ps_dc", bufs=3))
        ps_q = ctx.enter_context(tc.psum_pool(name="ps_q", bufs=1))

        xv = x_bytes.rearrange("(p i) k -> p i k", i=TILES)
        cv = cond.rearrange("(p i) k -> p i k", i=TILES)
        dv = delta_prev.rearrange("(p i) k -> p i k", i=TILES)
        ov = out.rearrange("(p i) k -> p i k", i=TILES)

        ctx.enter_context(tc.manual_schedule())

        def chunk_tiles(sizes, dtype, tag):
            where = []
            chunks = []
            first = 0
            for n, size in enumerate(sizes):
                chunk = keep.tile([P, size, D], dtype, name=tag + str(n))
                chunks.append((chunk, first, size))
                for j in range(size):
                    where.append((chunk, j))
                first += size
            return chunks, where

        x_chunks, x_at = chunk_tiles(X_CHUNKS, U8, "xb")
        c_chunks, c_at = chunk_tiles(C_CHUNKS, BF16, "cd")
        d_chunks, d_at = chunk_tiles(DP_CHUNKS, BF16, "dp")

        def load(chunks, view, n):
            chunk, first, size = chunks[n]
            nc.sync.dma_start(out=chunk[:], in_=view[:, first : first + size, :])

        def load_weight(w, tag):
            raw = keep.tile([P, T, F], BF16, name=tag + "_raw")
            nc.sync.dma_start(out=raw[:], in_=w.rearrange("(p j) n -> p j n", j=T))
            return raw

        scale = keep.tile([P, T], F32, name="scale")
        rad = keep.tile([P, TILES], BF16, name="rad")

        load(x_chunks, xv, 0)
        load(c_chunks, cv, 0)
        nc.sync.dma_start(out=scale[:], in_=x_scale.rearrange("o (p t) -> p (o t)", t=T))
        wc_raw = load_weight(wc, "wc")
        w1_raw = load_weight(w1, "w1")
        load(c_chunks, cv, 1)
        w2_raw = load_weight(w2, "w2")
        load(c_chunks, cv, 2)
        load(d_chunks, dv, 0)
        nc.sync.dma_start(out=rad[:], in_=radius.rearrange("(p i) -> p i", i=TILES))
        load(c_chunks, cv, 3)
        load(x_chunks, xv, 1)
        load(d_chunks, dv, 1)
        load(d_chunks, dv, 2)
        for n in range(4, 7):
            load(c_chunks, cv, n)
            load(x_chunks, xv, n - 2)
            load(d_chunks, dv, n - 1)

        ident = keep.tile([P, P], F32, name="ident")
        make_identity(nc, ident[:])
        expo = keep.tile([P, 2], F32, name="expo")
        nc.gpsimd.memset(expo[:, 0:1], -0.5)
        nc.gpsimd.memset(expo[:, 1:2], -1.0)
        rad3 = keep.tile([P, TILES], F32, name="rad3")

        warm_in = keep.tile([P, 1], F32, name="warm_in")
        warm_out = keep.tile([P, 1], F32, name="warm_out")
        nc.vector.memset(warm_in[:], 0.0)
        nc.scalar.activation(out=warm_out[:], in_=warm_in[:], func=ACT.Tanh)

        def weight_tiles(tag):
            grouped = keep.tile([P, F * T], BF16, name=tag + "_grp", align_bytes=64)
            codes = keep.tile([P, F], U32, name=tag + "_codes", align_bytes=64)
            scales = keep.tile([P, F], U8, name=tag + "_scales", align_bytes=64)
            return grouped, codes, scales

        def group_weight(raw, grouped, permuted):
            if permuted:
                dst = grouped[:].rearrange("p (t m j) -> p t m j", t=T, j=T)
                src = raw[:].rearrange("p j (m t) -> p t m j", t=T)
            else:
                dst = grouped[:].rearrange("p (h m j) -> p h m j", h=T, j=T)
                src = raw[:].rearrange("p j (h m) -> p h m j", h=T)
            return dst, src

        def group_on_v(pair, lo, hi):
            nc.vector.tensor_copy(out=pair[0][:, :, lo:hi], in_=pair[1][:, :, lo:hi])

        def group_on_s(pair, lo, hi):
            nc.scalar.copy(out=pair[0][:, :, lo:hi], in_=pair[1][:, :, lo:hi])

        def quantize(grouped, codes, scales):
            nc.vector.quantize_mx(out=codes[:].bitcast(FP8X4), scales=scales[:], in_=grouped[:])

        wc_t = weight_tiles("wc")
        w1_t = weight_tiles("w1")
        w2_t = weight_tiles("w2")

        live = {}

        def widen(i):
            chunk, j = x_at[i]
            xw = work.tile([P, D], BF16, name="xw", bufs=4)
            nc.scalar.copy(out=xw[:], in_=chunk[:, j, :].bitcast(FP8))
            live["xw", i] = xw

        def turn(i):
            chunk, j = c_at[i]
            xx = ps_xx.tile([P, 2, P], F32, name="xx")
            xc = ps_xc.tile([P, 2, P], F32, name="xc")
            for turned, rows in ((xx, live["xw", i][:]), (xc, chunk[:, j, :])):
                words = rows.bitcast(F32)
                for u in range(2):
                    nc.tensor.transpose(turned[:, u, :], words[:, u::2], ident[:])
            live["xx", i] = xx
            live["xc", i] = xc

        def scale_x(i):
            nc.vector.tensor_tensor(
                out=live["gh", i - 2][:, 0, :].rearrange("p (r u e) -> p r u e", u=2, e=2),
                in0=live["xx", i][:].bitcast(BF16).rearrange("p u (r e) -> p r u e", e=2),
                in1=scale[:].rearrange("p (o u e) -> p o u e", o=1, u=2).to_broadcast([P, P, 2, 2]),
                op=ALU.mult,
            )

        def empty(i):
            nc.scalar.copy(
                out=live["gh", i - 2][:, 1, :].bitcast(F32).rearrange("p (r u) -> p r u", u=2),
                in_=live["xc", i][:].rearrange("p u r -> p r u"),
            )

        def quant(s):
            front = 0 <= s + 2 < TILES
            back = 0 <= s < TILES
            lo = 0 if front else 2
            hi = 4 if back else 2
            codes = work.tile([P, 4 * P], U32, name="codes", align_bytes=64)
            scales = work.tile([P, 4 * P], U8, name="scales", align_bytes=64)
            nc.vector.quantize_mx(
                out=codes[:, lo * P : hi * P].bitcast(FP8X4),
                scales=scales[:, lo * P : hi * P],
                in_=live["gh", s][:, lo:hi, :].rearrange("p h n -> p (h n)"),
            )
            live["codes", s] = (codes, scales)

        def new_gh(s):
            live["gh", s] = work.tile([P, 4, P * T], BF16, name="gh", align_bytes=64)

        def stage1(i):
            xq, xs = live["codes", i - 2]
            a = ps_a.tile([P, T, P], F32, name="a")
            live["a", i] = a
            u = ps_u.tile([P, T, P], F32, name="u")
            for acc, w, lo in ((a, wc_t, P), (u, w1_t, 0)):
                for t in range(T):
                    nc.tensor.matmul_mx(
                        out=acc[:, t, :],
                        lhsT=w[1][:, t * P : (t + 1) * P].bitcast(FP8X4),
                        lhsT_scale=w[2][:, t * P : (t + 1) * P],
                        rhs=xq[:, lo : lo + P].bitcast(FP8X4),
                        rhs_scale=xs[:, lo : lo + P],
                        start=True,
                        stop=True,
                    )
            live["u", i] = u

        def tanh(i):
            th = work.tile([P, P, T], F32, name="th")
            nc.scalar.activation(
                out=th[:], in_=live["a", i][:].rearrange("p t r -> p r t"), func=ACT.Tanh
            )
            live["th", i] = th

        def neg_u(i):
            nc.scalar.activation(
                out=live["gh", i][:, 3, :].rearrange("p (r t) -> p r t", t=T),
                in_=live["u", i][:].rearrange("p t r -> p r t"),
                func=ACT.Copy,
                scale=-1.0,
            )

        def modulate(i):
            nc.vector.scalar_tensor_tensor(
                out=live["gh", i][:, 2, :].rearrange("p (r t) -> p r t", t=T),
                in0=live["th", i][:],
                scalar=1.0,
                in1=live["u", i][:].rearrange("p t r -> p r t"),
                op0=ALU.add,
                op1=ALU.mult,
            )

        def stage2(i):
            hq, hs = live["codes", i]

            def product(acc, h, start, stop):
                nc.tensor.matmul_mx(
                    out=acc[:],
                    lhsT=hq[:, h * P : (h + 1) * P].bitcast(FP8X4),
                    lhsT_scale=hs[:, h * P : (h + 1) * P],
                    rhs=w2_t[1][:].bitcast(FP8X4),
                    rhs_scale=w2_t[2][:],
                    start=start,
                    stop=stop,
                )

            q = ps_q.tile([P, D], F32, name="q")
            dc = ps_dc.tile([P, D], F32, name="dc")
            product(dc, 2, True, True)
            product(q, 2, True, False)
            product(q, 3, False, True)
            live["dc", i] = dc
            live["q", i] = q

        def delta(i):
            chunk, j = d_at[i]
            dl = work.tile([P, D], F32, name="dl", bufs=5)
            nc.vector.scalar_tensor_tensor(
                out=dl[:],
                in0=chunk[:, j, :],
                scalar=-0.5,
                in1=live["q", i][:],
                op0=ALU.mult,
                op1=ALU.add,
            )
            live["dl", i] = dl

        def sum_dc(i):
            st = work.tile([P, 2], F32, name="st", bufs=5)
            live["st", i] = st
            sq = work.tile([P, D], F32, name="sq", bufs=2)
            nc.scalar.activation(
                out=sq[:], in_=live["dc", i][:], func=ACT.Square, accum_out=st[:, 1:2]
            )

        def sum_delta(i):
            sq = work.tile([P, D], F32, name="sq", bufs=2)
            nc.scalar.activation(
                out=sq[:], in_=live["dl", i][:], func=ACT.Square, accum_out=live["st", i][:, 0:1]
            )

        def sum_cross(i):
            pr = work.tile([P, D], F32, name="pr", bufs=2)
            kk = work.tile([P, 1], F32, name="kk", bufs=4)
            nc.vector.scalar_tensor_tensor(
                out=pr[:],
                in0=live["dc", i][:],
                scalar=live["pw", i][:, 1:2],
                in1=live["dl", i][:],
                op0=ALU.mult,
                op1=ALU.mult,
                accum_out=kk[:],
            )
            live["kk", i] = kk

        def steps(i):
            pw = work.tile([P, 2], F32, name="pw", bufs=5)
            nb = work.tile([P, 1], F32, name="nb", bufs=5)
            sd = work.tile([P, D], F32, name="sd")
            nc.gpsimd.tensor_tensor(out=pw[:], in0=live["st", i][:], in1=expo[:], op=ALU.pow)
            nc.gpsimd.tensor_scalar(
                out=nb[:],
                in0=pw[:, 0:1],
                scalar1=rad3[:, i : i + 1],
                scalar2=-3.0,
                op0=ALU.mult,
                op1=ALU.max,
            )
            if i < TILES - 1:
                nc.gpsimd.tensor_scalar(
                    out=sd[:], in0=live["dl", i][:], scalar1=nb[:], scalar2=0.0, op0=ALU.mult, op1=ALU.add
                )
            live["pw", i] = pw
            live["nb", i] = nb
            live["sd", i] = sd

        def keep_dc(i):
            aa = work.tile([P, 1], F32, name="aa", bufs=5)
            nc.scalar.activation(
                out=aa[:], in_=live["kk", i][:], func=ACT.Identity, scale=live["nb", i][:], bias=1.0
            )
            live["aa", i] = aa

        def combine_columns(i, ot, cols):
            nc.vector.scalar_tensor_tensor(
                out=ot[:, i % 2, cols],
                in0=live["dc", i][:, cols],
                scalar=live["aa", i][:],
                in1=live["sd", i][:, cols],
                op0=ALU.mult,
                op1=ALU.subtract,
            )

        def combine(i):
            if i % 2 == 0:
                live["ot", i // 2] = work.tile([P, 2, D], F32, name="ot", bufs=4)
            ot = live["ot", i // 2]
            if i == TILES - 1:
                halves = (slice(0, D // 2), slice(D // 2, D))
                for cols in halves:
                    nc.vector.tensor_scalar(
                        out=live["sd", i][:, cols],
                        in0=live["dl", i][:, cols],
                        scalar1=live["nb", i][:],
                        scalar2=None,
                        op0=ALU.mult,
                    )
                for cols in halves:
                    combine_columns(i, ot, cols)
                    nc.sync.dma_start(out=ov[:, i, cols], in_=ot[:, i % 2, cols])
                return
            combine_columns(i, ot, slice(0, D))
            if i == TILES - 2:
                nc.sync.dma_start(out=ov[:, i, :], in_=ot[:, i % 2, :])
            elif i % 2 == 1:
                nc.sync.dma_start(out=ov[:, i - 1 : i + 1, :], in_=ot[:])

        def at(stage, i):
            if 0 <= i < TILES:
                stage(i)

        wc_pair = group_weight(wc_raw, wc_t[0], True)
        w1_pair = group_weight(w1_raw, w1_t[0], True)
        w2_pair = group_weight(w2_raw, w2_t[0], False)
        widen(0)
        turn(0)
        widen(1)
        group_on_v(wc_pair, 0, 96)
        group_on_s(wc_pair, 96, P)
        new_gh(-2)
        scale_x(0)
        empty(0)
        group_on_v(w1_pair, 0, 96)
        group_on_s(w1_pair, 96, P)
        turn(1)
        widen(2)
        quant(-2)
        quantize(*wc_t)
        quantize(*w1_t)
        stage1(0)
        group_on_s(w2_pair, 32, P)
        new_gh(-1)
        scale_x(1)
        empty(1)
        new_gh(0)
        tanh(0)
        neg_u(0)
        turn(2)
        widen(3)
        group_on_v(w2_pair, 0, 32)
        quant(-1)
        quantize(*w2_t)
        nc.gpsimd.tensor_scalar(
            out=rad3[:], in0=rad[:], scalar1=-3.0, scalar2=0.0, op0=ALU.mult, op1=ALU.add
        )
        for s in range(TILES + 3):
            at(empty, s + 2)
            at(sum_dc, s - 1)
            at(steps, s - 2)
            new_gh(s + 1)
            at(modulate, s)
            at(stage1, s + 1)
            at(tanh, s + 1)
            at(neg_u, s + 1)
            at(scale_x, s + 2)
            at(combine, s - 3)
            at(delta, s - 1)
            if s < TILES:
                quant(s)
            at(sum_cross, s - 2)
            at(sum_delta, s - 1)
            at(turn, s + 3)
            at(widen, s + 4)
            at(keep_dc, s - 2)
            at(stage2, s)
